import numpy as np
import ml_dtypes


def mxq(x, axis, fmt="e4m3"):
    dtype, down = {"e4m3": (ml_dtypes.float8_e4m3fn, 7), "e5m2": (ml_dtypes.float8_e5m2, 14)}[fmt]
    v = np.moveaxis(np.asarray(x, np.float32).astype(ml_dtypes.bfloat16).astype(np.float64), axis, -1)
    blocks = v.reshape(v.shape[:-1] + (-1, 32))
    amax = np.abs(blocks).max(-1, keepdims=True)
    byte = np.maximum(np.where(amax > 0, np.frexp(amax)[1] - 1 + 127, 0) - down, 1)
    scale = np.exp2(byte - 127.0)
    codes = (blocks / scale).astype(np.float32).astype(dtype).astype(np.float64)
    return np.moveaxis((codes * scale).reshape(v.shape), -1, axis)


WIDE = False


def mx_kscale(k):
    if not WIDE:
        return np.ones(k)
    levels = np.array([10, -10, 5, -5, 0])
    if k % 512:
        return np.exp2(np.random.permutation(np.resize(levels, k // 32))).repeat(32)
    a = np.empty((k // 512, 16))
    for p in range(k // 512):
        a[p, :8] = np.random.permutation(np.resize(levels, 8))
        for g in range(8):
            far = levels[np.abs(levels - a[p, g]) >= 10]
            a[p, g + 8] = far[np.random.randint(len(far))]
    return np.exp2(a.ravel()).repeat(32)


def f64(x):
    return np.asarray(x).astype(np.float64)


def striped8(idx):
    return np.asarray(idx).reshape(8, -1, 16).transpose(0, 2, 1).reshape(128, -1).astype(np.uint16)


def unstriped8(offs):
    return offs.reshape(8, 16, -1).transpose(0, 2, 1).reshape(8, -1).astype(np.int64)


def pick8(x, idx, run):
    r = np.arange(len(x))
    return x[r[:, None], idx[r % (8 * run) // run]]


E2M1 = np.array([0.0, 0.5, 1.0, 1.5, 2.0, 3.0, 4.0, 6.0, -0.0, -0.5, -1.0, -1.5, -2.0, -3.0, -4.0, -6.0])


def pack_weight(w, fmt):
    k, n = w.shape
    w = f64(np.asarray(w, np.float32).astype(ml_dtypes.bfloat16)).reshape(k // 32, 32, n)
    amax = np.abs(w).max(1)
    if fmt == "e4m3":
        byte = np.frexp(amax)[1] - 1 + 127 - 7
    else:
        mant, ex = np.frexp(amax / 6.0)
        byte = np.where(mant > 0.5, ex, ex - 1) + 127
    byte = np.clip(np.where(amax > 0, byte, 1), 1, 254)
    scaled = (w * np.exp2(127.0 - byte)[:, None, :]).reshape(k, n).astype(np.float32)
    by_word = np.ascontiguousarray(scaled.reshape(k // 512, 128, 4, n).transpose(0, 1, 3, 2))
    if fmt == "e4m3":
        words = by_word.astype(ml_dtypes.float8_e4m3fn).view(np.uint8)
    else:
        c = by_word.astype(ml_dtypes.float4_e2m1fn).view(np.uint8) & 0xF
        words = (c[..., 0::2] | (c[..., 1::2] << 4)).reshape(k // 512, 128, 2 * n)
    return np.ascontiguousarray(words), np.ascontiguousarray(byte.astype(np.uint8).reshape(k // 512, 16, n))


def unpack_weight(words, scales, fmt):
    g, _, n = scales.shape
    words = np.ascontiguousarray(words).reshape(g, 128, n, -1)
    if fmt == "e4m3":
        vals = words.view(ml_dtypes.float8_e4m3fn).astype(np.float64)
    else:
        nib = np.empty((g, 128, n, 4), np.uint8)
        nib[..., 0::2] = words & 0xF
        nib[..., 1::2] = words >> 4
        vals = E2M1[nib]
    vals = vals * np.repeat(np.exp2(scales.astype(np.float64) - 127.0), 8, axis=1)[..., None]
    return vals.transpose(0, 1, 3, 2).reshape(g * 512, n)


def bf(x):
    return np.asarray(x, np.float32).astype(ml_dtypes.bfloat16)


def planes(Y):
    r, m = Y.shape
    b = f64(bf(Y)).reshape(r // 32, 32, m)
    amax = np.abs(b).max(1)
    byte = np.clip(np.where(amax > 0, np.frexp(amax)[1] - 1 + 127 - 7, 1), 1, 254)
    codes = (b * np.exp2(127.0 - byte)[:, None, :]).reshape(r, m).astype(np.float32).astype(ml_dtypes.float8_e4m3fn).view(np.uint8)
    words = codes.reshape(r // 512, 128, 4, m).transpose(0, 1, 3, 2)
    return np.ascontiguousarray(words), np.ascontiguousarray(byte.astype(np.uint8).reshape(r // 512, 16, m))


K, T, J, N = 512, 1024, 512, 512


def setup_inputs():
    n = np.random.standard_normal
    idx = np.stack([np.random.permutation(T)[:J] for _ in range(8)])
    fj = mx_kscale(J)
    tgp = pack_weight(n((J, N)) * fj[:, None], "e2m1")
    return {
        "xf": (n((K, T))).astype(np.float32),
        "rw": (np.random.uniform(0.5, 2.0, (1, J)) / fj).astype(np.float32),
        "tg_words": tgp[0],
        "tg_scales": tgp[1],
        "old": (1.0 * n((K, N))).astype(np.float32),
        "offs": striped8(idx),
    }


def reference(xf, rw, tg_words, tg_scales, old, offs):
    idx = unstriped8(offs)
    tgu = unpack_weight(tg_words, tg_scales, "e2m1")
    xs = pick8(f64(xf), idx, 64) * f64(rw)
    xj = xs.T
    xjq = mxq(xj, 0, "e4m3")
    w = xjq.T @ tgu
    y = 0.04 * w + 0.5 * f64(old)
    words, scales = planes(y)
    return y, words, scales

@@ -1,0 +1,159 @@
+from contextlib import ExitStack
+
+import concourse.mybir as mybir
+from concourse.masks import make_identity
+
+K, T, J, N = 512, 1024, 512, 512
+FLOPS = 2 * K * J * N
+
+F32 = mybir.dt.float32
+BF16 = mybir.dt.bfloat16
+I32 = mybir.dt.int32
+U32 = mybir.dt.uint32
+U16 = mybir.dt.uint16
+U8 = mybir.dt.uint8
+FP8X4 = mybir.dt.float8_e4m3fn_x4
+FP4X4 = mybir.dt.float4_e2m1fn_x4
+MULT = mybir.AluOpType.mult
+ADD = mybir.AluOpType.add
+
+P = 128
+PACK = 4
+HALF = N // 2
+SCALAR_COLS = 192
+
+
+def tile_list_head_tokens_to_weights_pl_kernel(tc, xf, rw, tg_words, tg_scales, old, offs, out_0, out_1, out_2):
+    nc = tc.nc
+    xf_rows = xf.rearrange("(p t) c -> p t c", t=PACK)
+    old_rows = old.rearrange("(p t) n -> p t n", t=PACK)
+    out_rows = out_0.rearrange("(p t) n -> p t n", t=PACK)
+    out_words = out_1[0].rearrange("p n r -> p (n r)").bitcast(I32)
+
+    with ExitStack() as ctx:
+        keep = ctx.enter_context(tc.tile_pool(name="keep", bufs=1))
+        psum = ctx.enter_context(tc.psum_pool(name="psum", bufs=1))
+
+        offsets = keep.tile([P, J // 16], U16, name="offsets")
+        nc.sync.dma_start(offsets[:], offs)
+        rw_cols = keep.tile([P, PACK], F32, name="rw_cols")
+        nc.scalar.dma_start(rw_cols[:], rw.rearrange("o (q s) -> (o q) s", s=PACK))
+        windows = []
+        for t in range(PACK):
+            window = keep.tile([P, T], F32, name="window%d" % t, tag="window%d" % t, align_bytes=64)
+            nc.sync.dma_start(window[:], xf_rows[:, t, :])
+            windows.append(window)
+
+        warm = keep.tile([P, 2], F32, name="warm")
+        nc.vector.memset(warm[:], 0.0)
+        nc.scalar.mul(warm[:, 1:2], warm[:, 0:1], 0.5)
+
+        tg_codes = keep.tile([P, 2 * N], U8, name="tg_codes", align_bytes=64)
+        tg_plane = keep.tile([P, N], U8, name="tg_plane", align_bytes=64)
+        nc.vector.memset(tg_plane[:].bitcast(U32), 0)
+        nc.sync.dma_start(tg_codes[:].bitcast(I32), tg_words[0].bitcast(I32))
+        for q in range(4):
+            nc.sync.dma_start(tg_plane[32 * q : 32 * q + 4, :].bitcast(I32), tg_scales[0, 4 * q : 4 * q + 4, :].bitcast(I32))
+        olds = []
+        for t in range(PACK):
+            old_t = keep.tile([P, N], F32, name="old%d" % t)
+            nc.sync.dma_start(old_t[:], old_rows[:, t, :])
+            olds.append(old_t)
+
+        ident = keep.tile([P, P], F32, name="ident")
+        make_identity(nc, ident[:])
+
+        rw_bank = psum.tile([P, PACK, P], F32, name="rw_bank")
+        for s in range(PACK):
+            nc.tensor.transpose(rw_bank[:, s, :], rw_cols[:, s : s + 1].to_broadcast([P, P]), ident[:])
+        rw_rows = keep.tile([P, J], F32, name="rw_rows")
+        nc.scalar.copy(rw_rows[:].rearrange("p (q s) -> p q s", s=PACK), rw_bank[:].rearrange("p s q -> p q s"))
+
+        y = keep.tile([P, PACK, N], F32, name="y")
+        y_grouped = keep.tile([P, N, PACK], BF16, name="y_grouped", align_bytes=64)
+        y_codes = keep.tile([P, N], U32, name="y_codes", align_bytes=64)
+        y_plane = keep.tile([P, N], U8, name="y_plane", align_bytes=64)
+
+        grouped = {}
+        sums = {}
+        halves = {}
+
+        def gather(t):
+            xs = keep.tile([P, J], F32, name="xs%d" % t)
+            nc.vector.tensor_tensor(xs[:], windows[t][:].indirect(offsets[:]), rw_rows[:], MULT)
+            pairs = keep.tile([P, 2, P, 2], BF16, name="pairs%d" % t)
+            nc.scalar.copy(pairs[:], xs[:].rearrange("p (q u e) -> p u q e", u=2, e=2))
+            words = pairs[:].rearrange("p u q e -> p (u q e)").bitcast(F32)
+            turned = psum.tile([P, 2, P], F32, name="turned%d" % t, tag="turned%d" % (t % 2))
+            for u in range(2):
+                nc.tensor.transpose(turned[:, u, :], words[:, u * P : (u + 1) * P], ident[:])
+            xj = keep.tile([P, P * PACK], BF16, name="xj%d" % t, align_bytes=64)
+            nc.scalar.copy(xj[:].bitcast(F32).rearrange("q (p u) -> q p u", u=2), turned[:].rearrange("q u p -> q p u"))
+            grouped[t] = xj
+
+        def multiply(t, ranges):
+            tag = "window2" if t == 0 else "codes%d" % t
+            codes = keep.tile([P, P], U32, name="codes%d" % t, tag=tag, align_bytes=64)
+            plane = keep.tile([P, P], U8, name="plane%d" % t, align_bytes=64)
+            nc.vector.quantize_mx(out=codes[:].bitcast(FP8X4), scales=plane[:], in_=grouped[t][:])
+            for n0, n1 in ranges:
+                acc = psum.tile([P, n1 - n0], F32, name="acc%d_%d" % (t, n0))
+                nc.tensor.matmul_mx(
+                    out=acc[:],
+                    lhsT=codes[:].bitcast(FP8X4),
+                    lhsT_scale=plane[:],
+                    rhs=tg_codes[:, 2 * n0 : 2 * n1].bitcast(FP4X4),
+                    rhs_scale=tg_plane[:, n0:n1],
+                    start=True,
+                    stop=True,
+                )
+                sums[t, n0] = acc
+
+        def halve(t):
+            half_old = keep.tile([P, N], F32, name="half_old%d" % t)
+            nc.scalar.mul(half_old[:], olds[t][:], 0.5)
+            halves[t] = half_old
+
+        def combine(t, ranges):
+            for n0, n1 in ranges:
+                nc.vector.scalar_tensor_tensor(y[:, t, n0:n1], sums[t, n0][:], 0.04, halves[t][:, n0:n1], MULT, ADD)
+            nc.sync.dma_start(out_rows[:, t, :], y[:, t, :])
+
+        def interleave(copy, n0, n1):
+            copy(
+                y_grouped[:, n0:n1, :].rearrange("p (c i) t -> p c t i", i=4),
+                y[:, :, n0:n1].rearrange("p t (c i) -> p c t i", i=4),
+            )
+
+        whole = [(0, N)]
+        split = [(0, HALF), (HALF, N)]
+        gather(0)
+        gather(1)
+        gather(2)
+        multiply(0, whole)
+        multiply(1, whole)
+        halve(0)
+        gather(3)
+        multiply(2, whole)
+        halve(1)
+        combine(0, whole)
+        halve(2)
+        combine(1, whole)
+        multiply(3, split)
+        halve(3)
+        combine(2, whole)
+        combine(3, split)
+
+        interleave(nc.scalar.copy, 0, SCALAR_COLS)
+        interleave(nc.vector.tensor_copy, SCALAR_COLS, HALF)
+        interleave(nc.vector.tensor_copy, HALF, N)
+        for n0, n1 in split:
+            nc.vector.quantize_mx(
+                out=y_codes[:, n0:n1].bitcast(FP8X4),
+                scales=y_plane[:, n0:n1],
+                in_=y_grouped[:, n0:n1, :].rearrange("p n t -> p (n t)"),
+            )
+            nc.sync.dma_start(out_words[:, n0:n1], y_codes[:, n0:n1].bitcast(I32))
+        for q in range(4):
+            queue = nc.scalar if q % 2 == 0 else nc.sync
+            queue.dma_start(out_2[0, 4 * q : 4 * q + 4, :].bitcast(I32), y_plane[32 * q : 32 * q + 4, :].bitcast(I32))

@@ -30,6 +30,9 @@ def tile_list_head_tokens_to_weights_pl_kernel(tc, xf, rw, tg_words, tg_scales, 
     out_rows = out_0.rearrange("(p t) n -> p t n", t=PACK)
     out_words = out_1[0].rearrange("p n r -> p (n r)").bitcast(I32)
 
+    whole = [(0, N)]
+    split = [(0, HALF), (HALF, N)]
+
     with ExitStack() as ctx:
         keep = ctx.enter_context(tc.tile_pool(name="keep", bufs=1))
         psum = ctx.enter_context(tc.psum_pool(name="psum", bufs=1))
@@ -38,8 +41,15 @@ def tile_list_head_tokens_to_weights_pl_kernel(tc, xf, rw, tg_words, tg_scales, 
         nc.sync.dma_start(offsets[:], offs)
         rw_cols = keep.tile([P, PACK], F32, name="rw_cols")
         nc.scalar.dma_start(rw_cols[:], rw.rearrange("o (q s) -> (o q) s", s=PACK))
+        tg_codes = keep.tile([P, 2 * N], U8, name="tg_codes", align_bytes=64)
+        tg_plane = keep.tile([P, N], U8, name="tg_plane", align_bytes=64)
+        nc.gpsimd.memset(tg_plane[:].bitcast(U32), 0)
         windows = []
         for t in range(PACK):
+            if t == PACK - 1:
+                nc.sync.dma_start(tg_codes[:].bitcast(I32), tg_words[0].bitcast(I32))
+                for q in range(4):
+                    nc.sync.dma_start(tg_plane[32 * q : 32 * q + 4, :].bitcast(I32), tg_scales[0, 4 * q : 4 * q + 4, :].bitcast(I32))
             window = keep.tile([P, T], F32, name="window%d" % t, tag="window%d" % t, align_bytes=64)
             nc.sync.dma_start(window[:], xf_rows[:, t, :])
             windows.append(window)
@@ -48,26 +58,24 @@ def tile_list_head_tokens_to_weights_pl_kernel(tc, xf, rw, tg_words, tg_scales, 
         nc.vector.memset(warm[:], 0.0)
         nc.scalar.mul(warm[:, 1:2], warm[:, 0:1], 0.5)
 
-        tg_codes = keep.tile([P, 2 * N], U8, name="tg_codes", align_bytes=64)
-        tg_plane = keep.tile([P, N], U8, name="tg_plane", align_bytes=64)
-        nc.vector.memset(tg_plane[:].bitcast(U32), 0)
-        nc.sync.dma_start(tg_codes[:].bitcast(I32), tg_words[0].bitcast(I32))
-        for q in range(4):
-            nc.sync.dma_start(tg_plane[32 * q : 32 * q + 4, :].bitcast(I32), tg_scales[0, 4 * q : 4 * q + 4, :].bitcast(I32))
         olds = []
-        for t in range(PACK):
-            old_t = keep.tile([P, N], F32, name="old%d" % t)
-            nc.sync.dma_start(old_t[:], old_rows[:, t, :])
-            olds.append(old_t)
+        for t in range(0, PACK, 2):
+            old_pair = keep.tile([P, 2, N], F32, name="old%d" % t)
+            nc.sync.dma_start(old_pair[:], old_rows[:, t : t + 2, :])
+            olds.append(old_pair)
 
         ident = keep.tile([P, P], F32, name="ident")
         make_identity(nc, ident[:])
 
-        rw_bank = psum.tile([P, PACK, P], F32, name="rw_bank")
+        rw_bank = psum.tile([P, PACK, P], F32, name="rw_bank", tag="turned0")
         for s in range(PACK):
             nc.tensor.transpose(rw_bank[:, s, :], rw_cols[:, s : s + 1].to_broadcast([P, P]), ident[:])
         rw_rows = keep.tile([P, J], F32, name="rw_rows")
-        nc.scalar.copy(rw_rows[:].rearrange("p (q s) -> p q s", s=PACK), rw_bank[:].rearrange("p s q -> p q s"))
+        for j0, j1 in split:
+            nc.scalar.copy(
+                rw_rows[:, j0:j1].rearrange("p (q s) -> p q s", s=PACK),
+                rw_bank[:, :, j0 // PACK : j1 // PACK].rearrange("p s q -> p q s"),
+            )
 
         y = keep.tile([P, PACK, N], F32, name="y")
         y_grouped = keep.tile([P, N, PACK], BF16, name="y_grouped", align_bytes=64)
@@ -76,30 +84,38 @@ def tile_list_head_tokens_to_weights_pl_kernel(tc, xf, rw, tg_words, tg_scales, 
 
         grouped = {}
         sums = {}
+        banks = {}
+        picked = {}
         halves = {}
 
-        def gather(t):
-            xs = keep.tile([P, J], F32, name="xs%d" % t)
-            nc.vector.tensor_tensor(xs[:], windows[t][:].indirect(offsets[:]), rw_rows[:], MULT)
-            pairs = keep.tile([P, 2, P, 2], BF16, name="pairs%d" % t)
-            nc.scalar.copy(pairs[:], xs[:].rearrange("p (q u e) -> p u q e", u=2, e=2))
-            words = pairs[:].rearrange("p u q e -> p (u q e)").bitcast(F32)
-            turned = psum.tile([P, 2, P], F32, name="turned%d" % t, tag="turned%d" % (t % 2))
+        def gather(t, ranges):
+            pairs = keep.tile([P, J], BF16, name="pairs%d" % t, tag="pairs%d" % (0 if t == 2 else t), align_bytes=64)
+            for j0, j1 in ranges:
+                tag = "xs%d_%d" % (t, j0)
+                if t == PACK - 1:
+                    tag = "pairs1" if j0 == 0 else "xj0"
+                xs = keep.tile([P, j1 - j0], F32, name="xs%d_%d" % (t, j0), tag=tag, align_bytes=64)
+                picks = windows[t][:].indirect(offsets[:, j0 // 16 : j1 // 16])
+                nc.vector.tensor_tensor(xs[:], picks, rw_rows[:, j0:j1], MULT)
+                nc.scalar.copy(pairs[:, j0:j1], xs[:])
+            words = pairs[:].bitcast(F32)
+            turned = psum.tile([P, 2, P], F32, name="turned%d" % t, tag="turned%d" % ((t + 1) % 3))
             for u in range(2):
-                nc.tensor.transpose(turned[:, u, :], words[:, u * P : (u + 1) * P], ident[:])
-            xj = keep.tile([P, P * PACK], BF16, name="xj%d" % t, align_bytes=64)
+                nc.tensor.transpose(turned[:, u, :], words[:, u : 2 * P : 2], ident[:])
+            xj = keep.tile([P, P * PACK], BF16, name="xj%d" % t, tag="xj%d" % t, align_bytes=64)
             nc.scalar.copy(xj[:].bitcast(F32).rearrange("q (p u) -> q p u", u=2), turned[:].rearrange("q u p -> q p u"))
             grouped[t] = xj
 
-        def multiply(t, ranges):
-            tag = "window2" if t == 0 else "codes%d" % t
-            codes = keep.tile([P, P], U32, name="codes%d" % t, tag=tag, align_bytes=64)
+        def multiply(t):
+            codes = keep.tile([P, P], U32, name="codes%d" % t, align_bytes=64)
             plane = keep.tile([P, P], U8, name="plane%d" % t, align_bytes=64)
             nc.vector.quantize_mx(out=codes[:].bitcast(FP8X4), scales=plane[:], in_=grouped[t][:])
-            for n0, n1 in ranges:
-                acc = psum.tile([P, n1 - n0], F32, name="acc%d_%d" % (t, n0))
+            acc = psum.tile([P, N], F32, name="acc%d" % t)
+            for n0, n1 in split:
+                if t == PACK - 1 and n0 > 0:
+                    acc = psum.tile([P, N], F32, name="acc_last")
                 nc.tensor.matmul_mx(
-                    out=acc[:],
+                    out=acc[:, n0:n1],
                     lhsT=codes[:].bitcast(FP8X4),
                     lhsT_scale=plane[:],
                     rhs=tg_codes[:, 2 * n0 : 2 * n1].bitcast(FP4X4),
@@ -109,14 +125,10 @@ def tile_list_head_tokens_to_weights_pl_kernel(tc, xf, rw, tg_words, tg_scales, 
                 )
                 sums[t, n0] = acc
 
-        def halve(t):
-            half_old = keep.tile([P, N], F32, name="half_old%d" % t)
-            nc.scalar.mul(half_old[:], olds[t][:], 0.5)
-            halves[t] = half_old
-
         def combine(t, ranges):
             for n0, n1 in ranges:
-                nc.vector.scalar_tensor_tensor(y[:, t, n0:n1], sums[t, n0][:], 0.04, halves[t][:, n0:n1], MULT, ADD)
+                half_old = halves[t][:, n0:n1]
+                nc.vector.scalar_tensor_tensor(y[:, t, n0:n1], sums[t, n0][:, n0:n1], 0.04, half_old, MULT, ADD)
             nc.sync.dma_start(out_rows[:, t, :], y[:, t, :])
 
         def interleave(copy, n0, n1):
@@ -125,24 +137,24 @@ def tile_list_head_tokens_to_weights_pl_kernel(tc, xf, rw, tg_words, tg_scales, 
                 y[:, :, n0:n1].rearrange("p t (c i) -> p c t i", i=4),
             )
 
-        whole = [(0, N)]
-        split = [(0, HALF), (HALF, N)]
-        gather(0)
-        gather(1)
-        gather(2)
-        multiply(0, whole)
-        multiply(1, whole)
-        halve(0)
-        gather(3)
-        multiply(2, whole)
-        halve(1)
-        combine(0, whole)
-        halve(2)
-        combine(1, whole)
-        multiply(3, split)
-        halve(3)
-        combine(2, whole)
-        combine(3, split)
+        gather(0, split)
+        gather(1, whole)
+        gather(2, whole)
+        multiply(0)
+        gather(3, split)
+        for t in range(1, PACK):
+            multiply(t)
+        early = keep.tile([P, 2, N], F32, name="half_old01", tag="xj1", align_bytes=64)
+        nc.vector.tensor_scalar_mul(early[:], olds[0][:], 0.5)
+        halves[0] = early[:, 0, :]
+        halves[1] = early[:, 1, :]
+        for t, tag in ((2, "xj0"), (3, "xj3")):
+            late = keep.tile([P, N], F32, name="half_old%d" % t, tag=tag, align_bytes=64)
+            for n0, n1 in split if t == PACK - 1 else whole:
+                nc.scalar.mul(late[:, n0:n1], olds[1][:, t - 2, n0:n1], 0.5)
+            halves[t] = late[:]
+        for t in range(PACK):
+            combine(t, split if t == PACK - 1 else whole)
 
         interleave(nc.scalar.copy, 0, SCALAR_COLS)
         interleave(nc.vector.tensor_copy, SCALAR_COLS, HALF)

from contextlib import ExitStack

import concourse.mybir as mybir
from concourse.masks import make_identity

K, T, J, N = 512, 1024, 512, 512
FLOPS = 2 * K * J * N

F32 = mybir.dt.float32
BF16 = mybir.dt.bfloat16
I32 = mybir.dt.int32
U32 = mybir.dt.uint32
U16 = mybir.dt.uint16
U8 = mybir.dt.uint8
FP8X4 = mybir.dt.float8_e4m3fn_x4
FP4X4 = mybir.dt.float4_e2m1fn_x4
MULT = mybir.AluOpType.mult
ADD = mybir.AluOpType.add

P = 128
PACK = 4
HALF = N // 2
SCALAR_COLS = 192


def tile_list_head_tokens_to_weights_pl_kernel(tc, xf, rw, tg_words, tg_scales, old, offs, out_0, out_1, out_2):
    nc = tc.nc
    xf_rows = xf.rearrange("(p t) c -> p t c", t=PACK)
    old_rows = old.rearrange("(p t) n -> p t n", t=PACK)
    out_rows = out_0.rearrange("(p t) n -> p t n", t=PACK)
    out_words = out_1[0].rearrange("p n r -> p (n r)").bitcast(I32)

    whole = [(0, N)]
    split = [(0, HALF), (HALF, N)]

    with ExitStack() as ctx:
        keep = ctx.enter_context(tc.tile_pool(name="keep", bufs=1))
        psum = ctx.enter_context(tc.psum_pool(name="psum", bufs=1))

        offsets = keep.tile([P, J // 16], U16, name="offsets")
        nc.sync.dma_start(offsets[:], offs)
        rw_cols = keep.tile([P, PACK], F32, name="rw_cols")
        nc.scalar.dma_start(rw_cols[:], rw.rearrange("o (q s) -> (o q) s", s=PACK))
        tg_codes = keep.tile([P, 2 * N], U8, name="tg_codes", align_bytes=64)
        tg_plane = keep.tile([P, N], U8, name="tg_plane", align_bytes=64)
        nc.gpsimd.memset(tg_plane[:].bitcast(U32), 0)
        windows = []
        for t in range(PACK):
            if t == PACK - 1:
                nc.sync.dma_start(tg_codes[:].bitcast(I32), tg_words[0].bitcast(I32))
                for q in range(4):
                    nc.sync.dma_start(tg_plane[32 * q : 32 * q + 4, :].bitcast(I32), tg_scales[0, 4 * q : 4 * q + 4, :].bitcast(I32))
            window = keep.tile([P, T], F32, name="window%d" % t, tag="window%d" % t, align_bytes=64)
            nc.sync.dma_start(window[:], xf_rows[:, t, :])
            windows.append(window)

        warm = keep.tile([P, 2], F32, name="warm")
        nc.vector.memset(warm[:], 0.0)
        nc.scalar.mul(warm[:, 1:2], warm[:, 0:1], 0.5)

        olds = []
        for t in range(0, PACK, 2):
            old_pair = keep.tile([P, 2, N], F32, name="old%d" % t)
            nc.sync.dma_start(old_pair[:], old_rows[:, t : t + 2, :])
            olds.append(old_pair)

        ident = keep.tile([P, P], F32, name="ident")
        make_identity(nc, ident[:])

        rw_bank = psum.tile([P, PACK, P], F32, name="rw_bank", tag="turned0")
        for s in range(PACK):
            nc.tensor.transpose(rw_bank[:, s, :], rw_cols[:, s : s + 1].to_broadcast([P, P]), ident[:])
        rw_rows = keep.tile([P, J], F32, name="rw_rows")
        for j0, j1 in split:
            nc.scalar.copy(
                rw_rows[:, j0:j1].rearrange("p (q s) -> p q s", s=PACK),
                rw_bank[:, :, j0 // PACK : j1 // PACK].rearrange("p s q -> p q s"),
            )

        y = keep.tile([P, PACK, N], F32, name="y")
        y_grouped = keep.tile([P, N, PACK], BF16, name="y_grouped", align_bytes=64)
        y_codes = keep.tile([P, N], U32, name="y_codes", align_bytes=64)
        y_plane = keep.tile([P, N], U8, name="y_plane", align_bytes=64)

        grouped = {}
        sums = {}
        banks = {}
        picked = {}
        halves = {}

        def gather(t, ranges):
            pairs = keep.tile([P, J], BF16, name="pairs%d" % t, tag="pairs%d" % (0 if t == 2 else t), align_bytes=64)
            for j0, j1 in ranges:
                tag = "xs%d_%d" % (t, j0)
                if t == PACK - 1:
                    tag = "pairs1" if j0 == 0 else "xj0"
                xs = keep.tile([P, j1 - j0], F32, name="xs%d_%d" % (t, j0), tag=tag, align_bytes=64)
                picks = windows[t][:].indirect(offsets[:, j0 // 16 : j1 // 16])
                nc.vector.tensor_tensor(xs[:], picks, rw_rows[:, j0:j1], MULT)
                nc.scalar.copy(pairs[:, j0:j1], xs[:])
            words = pairs[:].bitcast(F32)
            turned = psum.tile([P, 2, P], F32, name="turned%d" % t, tag="turned%d" % ((t + 1) % 3))
            for u in range(2):
                nc.tensor.transpose(turned[:, u, :], words[:, u : 2 * P : 2], ident[:])
            xj = keep.tile([P, P * PACK], BF16, name="xj%d" % t, tag="xj%d" % t, align_bytes=64)
            nc.scalar.copy(xj[:].bitcast(F32).rearrange("q (p u) -> q p u", u=2), turned[:].rearrange("q u p -> q p u"))
            grouped[t] = xj

        def multiply(t):
            codes = keep.tile([P, P], U32, name="codes%d" % t, align_bytes=64)
            plane = keep.tile([P, P], U8, name="plane%d" % t, align_bytes=64)
            nc.vector.quantize_mx(out=codes[:].bitcast(FP8X4), scales=plane[:], in_=grouped[t][:])
            acc = psum.tile([P, N], F32, name="acc%d" % t)
            for n0, n1 in split:
                if t == PACK - 1 and n0 > 0:
                    acc = psum.tile([P, N], F32, name="acc_last")
                nc.tensor.matmul_mx(
                    out=acc[:, n0:n1],
                    lhsT=codes[:].bitcast(FP8X4),
                    lhsT_scale=plane[:],
                    rhs=tg_codes[:, 2 * n0 : 2 * n1].bitcast(FP4X4),
                    rhs_scale=tg_plane[:, n0:n1],
                    start=True,
                    stop=True,
                )
                sums[t, n0] = acc

        def combine(t, ranges):
            for n0, n1 in ranges:
                half_old = halves[t][:, n0:n1]
                nc.vector.scalar_tensor_tensor(y[:, t, n0:n1], sums[t, n0][:, n0:n1], 0.04, half_old, MULT, ADD)
            nc.sync.dma_start(out_rows[:, t, :], y[:, t, :])

        def interleave(copy, n0, n1):
            copy(
                y_grouped[:, n0:n1, :].rearrange("p (c i) t -> p c t i", i=4),
                y[:, :, n0:n1].rearrange("p t (c i) -> p c t i", i=4),
            )

        gather(0, split)
        gather(1, whole)
        gather(2, whole)
        multiply(0)
        gather(3, split)
        for t in range(1, PACK):
            multiply(t)
        early = keep.tile([P, 2, N], F32, name="half_old01", tag="xj1", align_bytes=64)
        nc.vector.tensor_scalar_mul(early[:], olds[0][:], 0.5)
        halves[0] = early[:, 0, :]
        halves[1] = early[:, 1, :]
        for t, tag in ((2, "xj0"), (3, "xj3")):
            late = keep.tile([P, N], F32, name="half_old%d" % t, tag=tag, align_bytes=64)
            for n0, n1 in split if t == PACK - 1 else whole:
                nc.scalar.mul(late[:, n0:n1], olds[1][:, t - 2, n0:n1], 0.5)
            halves[t] = late[:]
        for t in range(PACK):
            combine(t, split if t == PACK - 1 else whole)

        interleave(nc.scalar.copy, 0, SCALAR_COLS)
        interleave(nc.vector.tensor_copy, SCALAR_COLS, HALF)
        interleave(nc.vector.tensor_copy, HALF, N)
        for n0, n1 in split:
            nc.vector.quantize_mx(
                out=y_codes[:, n0:n1].bitcast(FP8X4),
                scales=y_plane[:, n0:n1],
                in_=y_grouped[:, n0:n1, :].rearrange("p n t -> p (n t)"),
            )
            nc.sync.dma_start(out_words[:, n0:n1], y_codes[:, n0:n1].bitcast(I32))
        for q in range(4):
            queue = nc.scalar if q % 2 == 0 else nc.sync
            queue.dma_start(out_2[0, 4 * q : 4 * q + 4, :].bitcast(I32), y_plane[32 * q : 32 * q + 4, :].bitcast(I32))
